import numpy as np
import ml_dtypes


def mxq(x, axis, fmt="e4m3"):
    dtype, down = {"e4m3": (ml_dtypes.float8_e4m3fn, 7), "e5m2": (ml_dtypes.float8_e5m2, 14)}[fmt]
    v = np.moveaxis(np.asarray(x, np.float32).astype(ml_dtypes.bfloat16).astype(np.float64), axis, -1)
    blocks = v.reshape(v.shape[:-1] + (-1, 32))
    amax = np.abs(blocks).max(-1, keepdims=True)
    byte = np.maximum(np.where(amax > 0, np.frexp(amax)[1] - 1 + 127, 0) - down, 1)
    scale = np.exp2(byte - 127.0)
    codes = (blocks / scale).astype(np.float32).astype(dtype).astype(np.float64)
    return np.moveaxis((codes * scale).reshape(v.shape), -1, axis)


WIDE = False


def mx_kscale(k):
    if not WIDE:
        return np.ones(k)
    levels = np.array([10, -10, 5, -5, 0])
    if k % 512:
        return np.exp2(np.random.permutation(np.resize(levels, k // 32))).repeat(32)
    a = np.empty((k // 512, 16))
    for p in range(k // 512):
        a[p, :8] = np.random.permutation(np.resize(levels, 8))
        for g in range(8):
            far = levels[np.abs(levels - a[p, g]) >= 10]
            a[p, g + 8] = far[np.random.randint(len(far))]
    return np.exp2(a.ravel()).repeat(32)


def f64(x):
    return np.asarray(x).astype(np.float64)


def striped(idx):
    return np.tile(np.asarray(idx).reshape(-1, 16).T, (8, 1)).astype(np.uint16)


def unstriped(offs):
    return offs[:16].T.reshape(-1).astype(np.int64)


def striped8(idx):
    return np.asarray(idx).reshape(8, -1, 16).transpose(0, 2, 1).reshape(128, -1).astype(np.uint16)


def unstriped8(offs):
    return offs.reshape(8, 16, -1).transpose(0, 2, 1).reshape(8, -1).astype(np.int64)


def pick8(x, idx, run):
    r = np.arange(len(x))
    return x[r[:, None], idx[r % (8 * run) // run]]


E2M1 = np.array([0.0, 0.5, 1.0, 1.5, 2.0, 3.0, 4.0, 6.0, -0.0, -0.5, -1.0, -1.5, -2.0, -3.0, -4.0, -6.0])


def pack_weight(w, fmt):
    k, n = w.shape
    w = f64(np.asarray(w, np.float32).astype(ml_dtypes.bfloat16)).reshape(k // 32, 32, n)
    amax = np.abs(w).max(1)
    if fmt == "e4m3":
        byte = np.frexp(amax)[1] - 1 + 127 - 7
    else:
        mant, ex = np.frexp(amax / 6.0)
        byte = np.where(mant > 0.5, ex, ex - 1) + 127
    byte = np.clip(np.where(amax > 0, byte, 1), 1, 254)
    scaled = (w * np.exp2(127.0 - byte)[:, None, :]).reshape(k, n).astype(np.float32)
    by_word = np.ascontiguousarray(scaled.reshape(k // 512, 128, 4, n).transpose(0, 1, 3, 2))
    if fmt == "e4m3":
        words = by_word.astype(ml_dtypes.float8_e4m3fn).view(np.uint8)
    else:
        c = by_word.astype(ml_dtypes.float4_e2m1fn).view(np.uint8) & 0xF
        words = (c[..., 0::2] | (c[..., 1::2] << 4)).reshape(k // 512, 128, 2 * n)
    return np.ascontiguousarray(words), np.ascontiguousarray(byte.astype(np.uint8).reshape(k // 512, 16, n))


def unpack_weight(words, scales, fmt):
    g, _, n = scales.shape
    words = np.ascontiguousarray(words).reshape(g, 128, n, -1)
    if fmt == "e4m3":
        vals = words.view(ml_dtypes.float8_e4m3fn).astype(np.float64)
    else:
        nib = np.empty((g, 128, n, 4), np.uint8)
        nib[..., 0::2] = words & 0xF
        nib[..., 1::2] = words >> 4
        vals = E2M1[nib]
    vals = vals * np.repeat(np.exp2(scales.astype(np.float64) - 127.0), 8, axis=1)[..., None]
    return vals.transpose(0, 1, 3, 2).reshape(g * 512, n)


K, J, R, T, F, O, C, D, N, U = 512, 512, 512, 1024, 1024, 192, 256, 512, 256, 512


def setup_inputs():
    n = np.random.standard_normal
    idx = np.random.permutation(T)[:J]
    idx2 = np.stack([np.random.permutation(F)[:R] for _ in range(8)])
    idx3 = np.stack([np.random.permutation(J)[:O] for _ in range(8)])
    idx4 = np.stack([np.random.permutation(C)[:O] for _ in range(8)])
    idx5 = np.stack([np.random.permutation(D)[:C] for _ in range(8)])
    idx6 = np.stack([np.random.permutation(U)[:C] for _ in range(8)])
    idx7 = np.stack([np.random.permutation(U)[:C] for _ in range(8)])
    fk = mx_kscale(K)
    fr = mx_kscale(R)
    xtp = pack_weight(n((K, T)) * fk[:, None], "e4m3")
    wbp = pack_weight(n((R, N)) * 1 / np.sqrt(R) / fr[:, None], "e4m3")
    return {
        "xt_words": xtp[0],
        "xt_scales": xtp[1],
        "ua": (np.random.randint(-7, 8, (K, F)).astype(np.float64)).astype(np.float32),
        "ha": ((np.random.randint(8, 25, (K, 1)) / 1024.0) / fk[:, None]).astype(np.float32),
        "tl": (np.random.randint(-7, 8, (R, D)).astype(np.float64)).astype(np.float32),
        "sa": (np.random.uniform(0.5, 1.6, (R, 1)) * fr[:, None]).astype(np.float32),
        "sl": ((np.random.randint(6, 19, (R, 1)) / 64.0) * fr[:, None]).astype(np.float32),
        "wb_words": wbp[0],
        "wb_scales": wbp[1],
        "offs": striped(idx),
        "offs2": striped8(idx2),
        "offs3": striped8(idx3),
        "offs4": striped8(idx4),
        "offs5": striped8(idx5),
        "offs6": striped8(idx6),
        "offs7": striped8(idx7),
    }


def reference(xt_words, xt_scales, ua, ha, tl, sa, sl, wb_words, wb_scales, offs, offs2, offs3, offs4, offs5, offs6, offs7):
    idx = unstriped(offs)
    idx2 = unstriped8(offs2)
    idx3 = unstriped8(offs3)
    idx4 = unstriped8(offs4)
    idx5 = unstriped8(offs5)
    idx6 = unstriped8(offs6)
    idx7 = unstriped8(offs7)
    xtu = unpack_weight(xt_words, xt_scales, "e4m3")
    wbu = unpack_weight(wb_words, wb_scales, "e4m3")
    wc = pick8(f64(ua), idx2, 64) * f64(ha)
    wcq = mxq(wc, 0, "e4m3")
    xtidxg = xtu[:, idx]
    a = wcq.T @ xtidxg
    h1 = pick8(a, idx3, 64) * f64(sa)
    pw = np.zeros((R, C))
    pw[np.arange(R)[:, None], idx4[np.arange(R) % 512 // 64]] = h1
    hid = np.maximum(pw, pick8(f64(tl), idx5, 64) * f64(sl))
    hidq = mxq(hid, 0, "e4m3")
    p = wbu.T @ hidq
    m0 = np.maximum(p, 0.0)
    m1 = np.maximum(-p, 0.0)
    m2 = np.zeros((N, U))
    m2[np.arange(N)[:, None], idx6[np.arange(N) % 128 // 16]] = m0
    m3 = np.zeros((N, U))
    m3[np.arange(N)[:, None], idx7[np.arange(N) % 128 // 16]] = m1
    y = m2 - m3
    return y

@@ -1,0 +1,168 @@
+from contextlib import ExitStack
+
+import concourse.mybir as mybir
+
+K, J, R, T, F, O, C, D, N, U = 512, 512, 512, 1024, 1024, 192, 256, 512, 256, 512
+FLOPS = 2 * K * R * J + 2 * R * N * C
+
+F32 = mybir.dt.float32
+BF16 = mybir.dt.bfloat16
+I32 = mybir.dt.int32
+U32 = mybir.dt.uint32
+U16 = mybir.dt.uint16
+U8 = mybir.dt.uint8
+FP8X4 = mybir.dt.float8_e4m3fn_x4
+COPY = mybir.ActivationFunctionType.Copy
+ALU = mybir.AluOpType
+
+P = 128
+PACK = 4
+HEAD = 64
+
+
+def tile_picked_tokens_codes_one_holefill_one_endsplit_kernel(
+    tc, xt_words, xt_scales, ua, ha, tl, sa, sl, wb_words, wb_scales, offs, offs2, offs3, offs4, offs5, offs6, offs7, out
+):
+    nc = tc.nc
+    with ExitStack() as ctx:
+        lists = ctx.enter_context(tc.tile_pool(name="lists", bufs=1))
+        sb = ctx.enter_context(tc.tile_pool(name="sb", bufs=1))
+        psum = ctx.enter_context(tc.psum_pool(name="psum", bufs=1))
+
+        def load_list(src, name):
+            t = lists.tile(list(src.shape), U16, name=name)
+            nc.sync.dma_start(t[:], src)
+            return t
+
+        def load_column(queue, src, name):
+            t = sb.tile([P, PACK], F32, name=name)
+            queue.dma_start(out=t[:], in_=src.rearrange("(p t) o -> p (t o)", t=PACK))
+            return t
+
+        def load_rows(src, t, name):
+            rows = sb.tile([P, src.shape[1]], F32, name=name)
+            nc.sync.dma_start(out=rows[:], in_=src.rearrange("(p t) f -> t p f", t=PACK)[t])
+            return rows
+
+        def load_words(src, name):
+            words = sb.tile([P, src.shape[2]], I32, name=name, align_bytes=64)
+            nc.sync.dma_start(out=words[:], in_=src[0].rearrange("p c r -> p (c r)").bitcast(I32))
+            return words
+
+        def load_scale_rows(src, name):
+            staged = sb.tile([PACK, PACK, src.shape[2] // 4], I32, name=name)
+            nc.gpsimd.dma_start(out=staged[:], in_=src[0].bitcast(I32).rearrange("(q i) c -> i q c", i=PACK))
+            return staged
+
+        def spread_scale_rows(staged, name):
+            plane = sb.tile([P, staged.shape[2] * 4], U8, name=name, align_bytes=64)
+            nc.vector.memset(plane[:].bitcast(I32), 0)
+            for q in range(PACK):
+                nc.vector.tensor_copy(out=plane[32 * q : 32 * q + PACK, :].bitcast(I32), in_=staged[:, q, :])
+            return plane
+
+        def cleared(width, name):
+            page = sb.tile([P, width], F32, name=name)
+            nc.vector.memset(page[:], 0.0)
+            return page
+
+        ua_rows = [load_rows(ua, 0, "ua0")]
+        l2 = load_list(offs2, "l2")
+        ha_t = load_column(nc.sync, ha, "ha_t")
+        ua_rows.extend(load_rows(ua, t, "ua%d" % t) for t in range(1, PACK))
+        l1 = load_list(offs, "l1")
+        xw = load_words(xt_words, "xw")
+        l5 = load_list(offs5, "l5")
+        tl_rows = [load_rows(tl, t, "tl%d" % t) for t in range(PACK)]
+        l3 = load_list(offs3, "l3")
+        l4 = load_list(offs4, "l4")
+        ww = load_words(wb_words, "ww")
+        l6 = load_list(offs6, "l6")
+        l7 = load_list(offs7, "l7")
+        xs_staged = load_scale_rows(xt_scales, "xs_staged")
+        sl_t = load_column(nc.gpsimd, sl, "sl_t")
+        sa_t = load_column(nc.gpsimd, sa, "sa_t")
+        ws_staged = load_scale_rows(wb_scales, "ws_staged")
+
+        pw = [cleared(C, "pw%d" % t) for t in range(PACK)]
+        m2 = [cleared(U, "m2_%d" % b) for b in range(N // P)]
+        m3 = [cleared(U, "m3_%d" % b) for b in range(N // P)]
+        xs = spread_scale_rows(xs_staged, "xs")
+        xs_g = sb.tile([P, J], U8, name="xs_g", align_bytes=64)
+        nc.vector.tensor_copy(out=xs_g[:], in_=xs[:].indirect(l1[:]))
+        ws = spread_scale_rows(ws_staged, "ws")
+
+        wc = sb.tile([P, PACK, R], BF16, name="wc")
+        for t in range(PACK):
+            nc.scalar.activation(out=wc[:, t, :], in_=ua_rows[t][:].indirect(l2[:]), func=COPY, scale=ha_t[:, t : t + 1])
+
+        xw_g = sb.tile([P, J], U32, name="xw_g", align_bytes=64)
+        nc.vector.tensor_copy(out=xw_g[:], in_=xw[:].bitcast(U32).indirect(l1[:]))
+
+        level = []
+        for t in range(PACK):
+            lv = sb.tile([P, C], F32, name="level%d" % t)
+            nc.scalar.activation(out=lv[:], in_=tl_rows[t][:].indirect(l5[:]), func=COPY, scale=sl_t[:, t : t + 1])
+            level.append(lv)
+
+        wc_dealt = wc[:].rearrange("p k (m t) -> p t m k", t=PACK)
+        a_rows = []
+        for t in range(PACK):
+            woven = sb.tile([P, P, PACK], BF16, name="woven%d" % t, align_bytes=64)
+            nc.vector.tensor_copy(out=woven[:], in_=wc_dealt[:, t])
+            codes = sb.tile([P, P], U32, name="wc_codes%d" % t, align_bytes=64)
+            scales = sb.tile([P, P], U8, name="wc_scales%d" % t, align_bytes=64)
+            nc.vector.quantize_mx(out=codes[:].bitcast(FP8X4), scales=scales[:], in_=woven[:].rearrange("p m k -> p (m k)"))
+            bank = psum.tile([P, J], F32, name="a_bank%d" % t)
+            nc.tensor.matmul_mx(
+                out=bank[:], lhsT=codes[:].bitcast(FP8X4), lhsT_scale=scales[:], rhs=xw_g[:].bitcast(FP8X4), rhs_scale=xs_g[:], start=True, stop=True
+            )
+            rows = sb.tile([P, J], F32, name="a_rows%d" % t)
+            nc.vector.tensor_copy(out=rows[:], in_=bank[:])
+            a_rows.append(rows)
+
+        parts = [(0, HEAD, [(0, HEAD)]), (HEAD, C, [(0, 64), (64, 192)])]
+        hid = [sb.tile([P, c1 - c0, PACK], BF16, name="hid%d" % c0, align_bytes=64) for c0, c1, runs in parts]
+        for t in range(PACK):
+            h1 = sb.tile([P, O], F32, name="h1_%d" % t)
+            nc.scalar.activation(out=h1[:], in_=a_rows[t][:].indirect(l3[:]), func=COPY, scale=sa_t[:, t : t + 1])
+            nc.scalar.activation(out=pw[t][:].indirect(l4[:]), in_=h1[:], func=COPY)
+            if t < PACK - 1:
+                for (c0, c1, runs), part in zip(parts, hid):
+                    nc.vector.tensor_tensor(out=part[:, :, t], in0=pw[t][:, c0:c1], in1=level[t][:, c0:c1], op=ALU.max)
+
+        last = PACK - 1
+        for (c0, c1, runs), part in zip(parts, hid):
+            width = c1 - c0
+            nc.vector.tensor_tensor(out=part[:, :, last], in0=pw[last][:, c0:c1], in1=level[last][:, c0:c1], op=ALU.max)
+            codes = sb.tile([P, width], U32, name="hid_codes%d" % c0, align_bytes=64)
+            scales = sb.tile([P, width], U8, name="hid_scales%d" % c0, align_bytes=64)
+            for r0, r1 in runs:
+                nc.vector.quantize_mx(
+                    out=codes[:, r0:r1].bitcast(FP8X4), scales=scales[:, r0:r1], in_=part[:, r0:r1, :].rearrange("p c t -> p (c t)")
+                )
+            for b in range(N // P):
+                bank = psum.tile([P, width], F32, name="p_bank%d_%d" % (c0, b))
+                for r0, r1 in runs:
+                    nc.tensor.matmul_mx(
+                        out=bank[:, r0:r1],
+                        lhsT=ww[:, b * P : (b + 1) * P].bitcast(FP8X4),
+                        lhsT_scale=ws[:, b * P : (b + 1) * P],
+                        rhs=codes[:, r0:r1].bitcast(FP8X4),
+                        rhs_scale=scales[:, r0:r1],
+                        start=True,
+                        stop=True,
+                    )
+                m0 = sb.tile([P, width], F32, name="m0_%d_%d" % (c0, b))
+                m1 = sb.tile([P, width], F32, name="m1_%d_%d" % (c0, b))
+                nc.vector.tensor_scalar_max(out=m0[:], in0=bank[:], scalar1=0.0)
+                nc.vector.tensor_scalar(out=m1[:], in0=bank[:], scalar1=-1.0, scalar2=0.0, op0=ALU.mult, op1=ALU.max)
+                nc.scalar.activation(out=m2[b][:].indirect(l6[:, c0 // 16 : c1 // 16]), in_=m0[:], func=COPY)
+                nc.scalar.activation(out=m3[b][:].indirect(l7[:, c0 // 16 : c1 // 16]), in_=m1[:], func=COPY)
+
+        for b in range(N // P):
+            for half, queue in enumerate((nc.sync, nc.scalar)):
+                cols = slice(half * U // 2, (half + 1) * U // 2)
+                y = sb.tile([P, U // 2], F32, name="y%d_%d" % (b, half))
+                nc.vector.tensor_sub(out=y[:], in0=m2[b][:, cols], in1=m3[b][:, cols])
+                (queue if b == N // P - 1 else nc.sync).dma_start(out=out[b * P : (b + 1) * P, cols], in_=y[:])

@@ -40,64 +40,90 @@ def tile_picked_tokens_codes_one_holefill_one_endsplit_kernel(
             return t
 
         def load_rows(src, t, name):
-            rows = sb.tile([P, src.shape[1]], F32, name=name)
+            rows = sb.tile([P, src.shape[1]], F32, name=name, tag=name)
             nc.sync.dma_start(out=rows[:], in_=src.rearrange("(p t) f -> t p f", t=PACK)[t])
             return rows
 
         def load_words(src, name):
-            words = sb.tile([P, src.shape[2]], I32, name=name, align_bytes=64)
+            words = sb.tile([P, src.shape[2]], I32, name=name, tag=name, align_bytes=64)
             nc.sync.dma_start(out=words[:], in_=src[0].rearrange("p c r -> p (c r)").bitcast(I32))
             return words
 
-        def load_scale_rows(src, name):
+        def load_scale_rows(queue, src, name):
             staged = sb.tile([PACK, PACK, src.shape[2] // 4], I32, name=name)
-            nc.gpsimd.dma_start(out=staged[:], in_=src[0].bitcast(I32).rearrange("(q i) c -> i q c", i=PACK))
+            queue.dma_start(out=staged[:], in_=src[0].bitcast(I32).rearrange("(q i) c -> i q c", i=PACK))
             return staged
 
-        def spread_scale_rows(staged, name):
-            plane = sb.tile([P, staged.shape[2] * 4], U8, name=name, align_bytes=64)
+        def spread_scale_rows(staged, name, tag):
+            plane = sb.tile([P, staged.shape[2] * 4], U8, name=name, tag=tag, align_bytes=64)
             nc.vector.memset(plane[:].bitcast(I32), 0)
             for q in range(PACK):
                 nc.vector.tensor_copy(out=plane[32 * q : 32 * q + PACK, :].bitcast(I32), in_=staged[:, q, :])
             return plane
 
-        def cleared(width, name):
-            page = sb.tile([P, width], F32, name=name)
+        def cleared(width, name, tag=None):
+            page = sb.tile([P, width], F32, name=name, tag=tag or name, align_bytes=64)
             nc.vector.memset(page[:], 0.0)
             return page
 
         ua_rows = [load_rows(ua, 0, "ua0")]
         l2 = load_list(offs2, "l2")
         ha_t = load_column(nc.sync, ha, "ha_t")
-        ua_rows.extend(load_rows(ua, t, "ua%d" % t) for t in range(1, PACK))
+        xs_staged = load_scale_rows(nc.sync, xt_scales, "xs_staged")
         l1 = load_list(offs, "l1")
+        ua_rows.extend(load_rows(ua, t, "ua%d" % t) for t in range(1, PACK - 1))
         xw = load_words(xt_words, "xw")
+        ua_rows.append(load_rows(ua, PACK - 1, "ua3"))
         l5 = load_list(offs5, "l5")
-        tl_rows = [load_rows(tl, t, "tl%d" % t) for t in range(PACK)]
         l3 = load_list(offs3, "l3")
         l4 = load_list(offs4, "l4")
+        sl_t = load_column(nc.gpsimd, sl, "sl_t")
+        tl_rows = [load_rows(tl, t, "tl%d" % t) for t in range(PACK)]
+        sa_t = load_column(nc.gpsimd, sa, "sa_t")
+        ws_staged = load_scale_rows(nc.gpsimd, wb_scales, "ws_staged")
         ww = load_words(wb_words, "ww")
         l6 = load_list(offs6, "l6")
         l7 = load_list(offs7, "l7")
-        xs_staged = load_scale_rows(xt_scales, "xs_staged")
-        sl_t = load_column(nc.gpsimd, sl, "sl_t")
-        sa_t = load_column(nc.gpsimd, sa, "sa_t")
-        ws_staged = load_scale_rows(wb_scales, "ws_staged")
 
         pw = [cleared(C, "pw%d" % t) for t in range(PACK)]
         m2 = [cleared(U, "m2_%d" % b) for b in range(N // P)]
         m3 = [cleared(U, "m3_%d" % b) for b in range(N // P)]
-        xs = spread_scale_rows(xs_staged, "xs")
-        xs_g = sb.tile([P, J], U8, name="xs_g", align_bytes=64)
+        xs = spread_scale_rows(xs_staged, "xs", "xs")
+        xs_g = sb.tile([P, J], U8, name="xs_g", tag="xs_g", align_bytes=64)
         nc.vector.tensor_copy(out=xs_g[:], in_=xs[:].indirect(l1[:]))
-        ws = spread_scale_rows(ws_staged, "ws")
 
-        wc = sb.tile([P, PACK, R], BF16, name="wc")
-        for t in range(PACK):
-            nc.scalar.activation(out=wc[:, t, :], in_=ua_rows[t][:].indirect(l2[:]), func=COPY, scale=ha_t[:, t : t + 1])
+        woven = sb.tile([P, PACK, P, PACK], BF16, name="woven", align_bytes=64)
 
-        xw_g = sb.tile([P, J], U32, name="xw_g", align_bytes=64)
+        def gather_codes(dst, k, r0, r1):
+            nc.scalar.activation(out=dst, in_=ua_rows[k][:].indirect(l2[:, r0 // 16 : r1 // 16]), func=COPY, scale=ha_t[:, k : k + 1])
+
+        def dealt(pair):
+            return pair[:].rearrange("p k (m t) -> p t m k", t=PACK)
+
+        wc_low = sb.tile([P, 2, R], BF16, name="wc_low")
+        wc_high = [sb.tile([P, 2, R // 2], BF16, name="wc_high%d" % half) for half in range(2)]
+        for k in range(2):
+            gather_codes(wc_low[:, k, :], k, 0, R)
+        nc.vector.tensor_copy(out=woven[:, :, :, 0:2], in_=dealt(wc_low))
+        xw_g = sb.tile([P, J], U32, name="xw_g", tag="xw_g", align_bytes=64)
         nc.vector.tensor_copy(out=xw_g[:], in_=xw[:].bitcast(U32).indirect(l1[:]))
+        for k in range(2, PACK):
+            for half in range(2):
+                gather_codes(wc_high[half][:, k - 2, :], k, half * R // 2, (half + 1) * R // 2)
+        nc.vector.tensor_copy(out=woven[:, :, : P // 2, 2:4], in_=dealt(wc_high[0]))
+
+        def quantise_wc(woven, t):
+            codes = sb.tile([P, P], U32, name="wc_codes%d" % t, tag="wc_codes%d" % t, align_bytes=64)
+            scales = sb.tile([P, P], U8, name="wc_scales%d" % t, tag="wc_scales%d" % t, align_bytes=64)
+            nc.vector.quantize_mx(out=codes[:].bitcast(FP8X4), scales=scales[:], in_=woven.rearrange("p m k -> p (m k)"))
+            return codes, scales
+
+        def first_product(wq, cols, tag):
+            bank = psum.tile([P, cols.stop - cols.start], F32, name="a_" + tag, tag=tag)
+            nc.tensor.matmul_mx(
+                out=bank[:], lhsT=wq[0][:].bitcast(FP8X4), lhsT_scale=wq[1][:], rhs=xw_g[:, cols].bitcast(FP8X4), rhs_scale=xs_g[:, cols], start=True, stop=True
+            )
+            return bank
 
         level = []
         for t in range(PACK):
@@ -105,44 +131,41 @@ def tile_picked_tokens_codes_one_holefill_one_endsplit_kernel(
             nc.scalar.activation(out=lv[:], in_=tl_rows[t][:].indirect(l5[:]), func=COPY, scale=sl_t[:, t : t + 1])
             level.append(lv)
 
-        wc_dealt = wc[:].rearrange("p k (m t) -> p t m k", t=PACK)
-        a_rows = []
+        a_rows = [sb.tile([P, J], F32, name="a_rows%d" % t) for t in range(PACK)]
         for t in range(PACK):
-            woven = sb.tile([P, P, PACK], BF16, name="woven%d" % t, align_bytes=64)
-            nc.vector.tensor_copy(out=woven[:], in_=wc_dealt[:, t])
-            codes = sb.tile([P, P], U32, name="wc_codes%d" % t, align_bytes=64)
-            scales = sb.tile([P, P], U8, name="wc_scales%d" % t, align_bytes=64)
-            nc.vector.quantize_mx(out=codes[:].bitcast(FP8X4), scales=scales[:], in_=woven[:].rearrange("p m k -> p (m k)"))
-            bank = psum.tile([P, J], F32, name="a_bank%d" % t)
-            nc.tensor.matmul_mx(
-                out=bank[:], lhsT=codes[:].bitcast(FP8X4), lhsT_scale=scales[:], rhs=xw_g[:].bitcast(FP8X4), rhs_scale=xs_g[:], start=True, stop=True
-            )
-            rows = sb.tile([P, J], F32, name="a_rows%d" % t)
-            nc.vector.tensor_copy(out=rows[:], in_=bank[:])
-            a_rows.append(rows)
+            nc.vector.tensor_copy(out=woven[:, t, P // 2 :, 2:4], in_=dealt(wc_high[1])[:, t])
+            wq = quantise_wc(woven[:, t], t)
+            pieces = [slice(0, J // 2), slice(J // 2, J)] if t == 0 else [slice(0, J)]
+            for cols in pieces:
+                bank = first_product(wq, cols, "bank%d" % (t if cols.start == 0 else PACK))
+                nc.vector.tensor_copy(out=a_rows[t][:, cols], in_=bank[:])
 
-        parts = [(0, HEAD, [(0, HEAD)]), (HEAD, C, [(0, 64), (64, 192)])]
-        hid = [sb.tile([P, c1 - c0, PACK], BF16, name="hid%d" % c0, align_bytes=64) for c0, c1, runs in parts]
+        ws = spread_scale_rows(ws_staged, "ws", "xw_g")
+        h1 = sb.tile([P, PACK, O], F32, name="h1", tag="tl3")
+        hid_head = sb.tile([P, HEAD, PACK], BF16, name="hid_head", align_bytes=64)
+        rest_planes = sb.tile([P, PACK, C - HEAD], BF16, name="rest_planes")
+
+        def gather_slots(t):
+            nc.scalar.activation(out=h1[:, t, :], in_=a_rows[t][:].indirect(l3[:]), func=COPY, scale=sa_t[:, t : t + 1])
+
+        gather_slots(0)
         for t in range(PACK):
-            h1 = sb.tile([P, O], F32, name="h1_%d" % t)
-            nc.scalar.activation(out=h1[:], in_=a_rows[t][:].indirect(l3[:]), func=COPY, scale=sa_t[:, t : t + 1])
-            nc.scalar.activation(out=pw[t][:].indirect(l4[:]), in_=h1[:], func=COPY)
-            if t < PACK - 1:
-                for (c0, c1, runs), part in zip(parts, hid):
-                    nc.vector.tensor_tensor(out=part[:, :, t], in0=pw[t][:, c0:c1], in1=level[t][:, c0:c1], op=ALU.max)
+            if t + 1 < PACK:
+                gather_slots(t + 1)
+            nc.scalar.activation(out=pw[t][:].indirect(l4[:]), in_=h1[:, t, :], func=COPY)
+            nc.vector.tensor_tensor(out=hid_head[:, :, t], in0=pw[t][:, :HEAD], in1=level[t][:, :HEAD], op=ALU.max)
+            nc.vector.tensor_tensor(out=rest_planes[:, t, :], in0=pw[t][:, HEAD:], in1=level[t][:, HEAD:], op=ALU.max)
 
-        last = PACK - 1
-        for (c0, c1, runs), part in zip(parts, hid):
+        def second_product(hid, c0, c1, runs, tags):
             width = c1 - c0
-            nc.vector.tensor_tensor(out=part[:, :, last], in0=pw[last][:, c0:c1], in1=level[last][:, c0:c1], op=ALU.max)
             codes = sb.tile([P, width], U32, name="hid_codes%d" % c0, align_bytes=64)
             scales = sb.tile([P, width], U8, name="hid_scales%d" % c0, align_bytes=64)
             for r0, r1 in runs:
                 nc.vector.quantize_mx(
-                    out=codes[:, r0:r1].bitcast(FP8X4), scales=scales[:, r0:r1], in_=part[:, r0:r1, :].rearrange("p c t -> p (c t)")
+                    out=codes[:, r0:r1].bitcast(FP8X4), scales=scales[:, r0:r1], in_=hid[:, r0:r1, :].rearrange("p c t -> p (c t)")
                 )
             for b in range(N // P):
-                bank = psum.tile([P, width], F32, name="p_bank%d_%d" % (c0, b))
+                bank = psum.tile([P, width], F32, name="p_bank%d_%d" % (c0, b), tag=tags[b])
                 for r0, r1 in runs:
                     nc.tensor.matmul_mx(
                         out=bank[:, r0:r1],
@@ -159,6 +182,11 @@ def tile_picked_tokens_codes_one_holefill_one_endsplit_kernel(
                 nc.vector.tensor_scalar(out=m1[:], in0=bank[:], scalar1=-1.0, scalar2=0.0, op0=ALU.mult, op1=ALU.max)
                 nc.scalar.activation(out=m2[b][:].indirect(l6[:, c0 // 16 : c1 // 16]), in_=m0[:], func=COPY)
                 nc.scalar.activation(out=m3[b][:].indirect(l7[:, c0 // 16 : c1 // 16]), in_=m1[:], func=COPY)
+
+        second_product(hid_head, 0, HEAD, [(0, HEAD)], ["bank5", "bank6"])
+        hid_rest = sb.tile([P, C - HEAD, PACK], BF16, name="hid_rest", align_bytes=64)
+        nc.vector.tensor_copy(out=hid_rest[:], in_=rest_planes[:].rearrange("p t c -> p c t"))
+        second_product(hid_rest, HEAD, C, [(0, 64), (64, 192)], ["bank7", "bank0"])
 
         for b in range(N // P):
             for half, queue in enumerate((nc.sync, nc.scalar)):

@@ -85,6 +85,9 @@ def tile_picked_tokens_codes_one_holefill_one_endsplit_kernel(
         l6 = load_list(offs6, "l6")
         l7 = load_list(offs7, "l7")
 
+        warm_in = cleared(8, "warm_in")
+        warm_out = sb.tile([P, 8], F32, name="warm_out")
+        nc.scalar.activation(out=warm_out[:], in_=warm_in[:], func=COPY)
         pw = [cleared(C, "pw%d" % t) for t in range(PACK)]
         m2 = [cleared(U, "m2_%d" % b) for b in range(N // P)]
         m3 = [cleared(U, "m3_%d" % b) for b in range(N // P)]

from contextlib import ExitStack

import concourse.mybir as mybir

K, J, R, T, F, O, C, D, N, U = 512, 512, 512, 1024, 1024, 192, 256, 512, 256, 512
FLOPS = 2 * K * R * J + 2 * R * N * C

F32 = mybir.dt.float32
BF16 = mybir.dt.bfloat16
I32 = mybir.dt.int32
U32 = mybir.dt.uint32
U16 = mybir.dt.uint16
U8 = mybir.dt.uint8
FP8X4 = mybir.dt.float8_e4m3fn_x4
COPY = mybir.ActivationFunctionType.Copy
ALU = mybir.AluOpType

P = 128
PACK = 4
HEAD = 64


def tile_picked_tokens_codes_one_holefill_one_endsplit_kernel(
    tc, xt_words, xt_scales, ua, ha, tl, sa, sl, wb_words, wb_scales, offs, offs2, offs3, offs4, offs5, offs6, offs7, out
):
    nc = tc.nc
    with ExitStack() as ctx:
        lists = ctx.enter_context(tc.tile_pool(name="lists", bufs=1))
        sb = ctx.enter_context(tc.tile_pool(name="sb", bufs=1))
        psum = ctx.enter_context(tc.psum_pool(name="psum", bufs=1))

        def load_list(src, name):
            t = lists.tile(list(src.shape), U16, name=name)
            nc.sync.dma_start(t[:], src)
            return t

        def load_column(queue, src, name):
            t = sb.tile([P, PACK], F32, name=name)
            queue.dma_start(out=t[:], in_=src.rearrange("(p t) o -> p (t o)", t=PACK))
            return t

        def load_rows(src, t, name):
            rows = sb.tile([P, src.shape[1]], F32, name=name, tag=name)
            nc.sync.dma_start(out=rows[:], in_=src.rearrange("(p t) f -> t p f", t=PACK)[t])
            return rows

        def load_words(src, name):
            words = sb.tile([P, src.shape[2]], I32, name=name, tag=name, align_bytes=64)
            nc.sync.dma_start(out=words[:], in_=src[0].rearrange("p c r -> p (c r)").bitcast(I32))
            return words

        def load_scale_rows(queue, src, name):
            staged = sb.tile([PACK, PACK, src.shape[2] // 4], I32, name=name)
            queue.dma_start(out=staged[:], in_=src[0].bitcast(I32).rearrange("(q i) c -> i q c", i=PACK))
            return staged

        def spread_scale_rows(staged, name, tag):
            plane = sb.tile([P, staged.shape[2] * 4], U8, name=name, tag=tag, align_bytes=64)
            nc.vector.memset(plane[:].bitcast(I32), 0)
            for q in range(PACK):
                nc.vector.tensor_copy(out=plane[32 * q : 32 * q + PACK, :].bitcast(I32), in_=staged[:, q, :])
            return plane

        def cleared(width, name, tag=None):
            page = sb.tile([P, width], F32, name=name, tag=tag or name, align_bytes=64)
            nc.vector.memset(page[:], 0.0)
            return page

        ua_rows = [load_rows(ua, 0, "ua0")]
        l2 = load_list(offs2, "l2")
        ha_t = load_column(nc.sync, ha, "ha_t")
        xs_staged = load_scale_rows(nc.sync, xt_scales, "xs_staged")
        l1 = load_list(offs, "l1")
        ua_rows.extend(load_rows(ua, t, "ua%d" % t) for t in range(1, PACK - 1))
        xw = load_words(xt_words, "xw")
        ua_rows.append(load_rows(ua, PACK - 1, "ua3"))
        l5 = load_list(offs5, "l5")
        l3 = load_list(offs3, "l3")
        l4 = load_list(offs4, "l4")
        sl_t = load_column(nc.gpsimd, sl, "sl_t")
        tl_rows = [load_rows(tl, t, "tl%d" % t) for t in range(PACK)]
        sa_t = load_column(nc.gpsimd, sa, "sa_t")
        ws_staged = load_scale_rows(nc.gpsimd, wb_scales, "ws_staged")
        ww = load_words(wb_words, "ww")
        l6 = load_list(offs6, "l6")
        l7 = load_list(offs7, "l7")

        warm_in = cleared(8, "warm_in")
        warm_out = sb.tile([P, 8], F32, name="warm_out")
        nc.scalar.activation(out=warm_out[:], in_=warm_in[:], func=COPY)
        pw = [cleared(C, "pw%d" % t) for t in range(PACK)]
        m2 = [cleared(U, "m2_%d" % b) for b in range(N // P)]
        m3 = [cleared(U, "m3_%d" % b) for b in range(N // P)]
        xs = spread_scale_rows(xs_staged, "xs", "xs")
        xs_g = sb.tile([P, J], U8, name="xs_g", tag="xs_g", align_bytes=64)
        nc.vector.tensor_copy(out=xs_g[:], in_=xs[:].indirect(l1[:]))

        woven = sb.tile([P, PACK, P, PACK], BF16, name="woven", align_bytes=64)

        def gather_codes(dst, k, r0, r1):
            nc.scalar.activation(out=dst, in_=ua_rows[k][:].indirect(l2[:, r0 // 16 : r1 // 16]), func=COPY, scale=ha_t[:, k : k + 1])

        def dealt(pair):
            return pair[:].rearrange("p k (m t) -> p t m k", t=PACK)

        wc_low = sb.tile([P, 2, R], BF16, name="wc_low")
        wc_high = [sb.tile([P, 2, R // 2], BF16, name="wc_high%d" % half) for half in range(2)]
        for k in range(2):
            gather_codes(wc_low[:, k, :], k, 0, R)
        nc.vector.tensor_copy(out=woven[:, :, :, 0:2], in_=dealt(wc_low))
        xw_g = sb.tile([P, J], U32, name="xw_g", tag="xw_g", align_bytes=64)
        nc.vector.tensor_copy(out=xw_g[:], in_=xw[:].bitcast(U32).indirect(l1[:]))
        for k in range(2, PACK):
            for half in range(2):
                gather_codes(wc_high[half][:, k - 2, :], k, half * R // 2, (half + 1) * R // 2)
        nc.vector.tensor_copy(out=woven[:, :, : P // 2, 2:4], in_=dealt(wc_high[0]))

        def quantise_wc(woven, t):
            codes = sb.tile([P, P], U32, name="wc_codes%d" % t, tag="wc_codes%d" % t, align_bytes=64)
            scales = sb.tile([P, P], U8, name="wc_scales%d" % t, tag="wc_scales%d" % t, align_bytes=64)
            nc.vector.quantize_mx(out=codes[:].bitcast(FP8X4), scales=scales[:], in_=woven.rearrange("p m k -> p (m k)"))
            return codes, scales

        def first_product(wq, cols, tag):
            bank = psum.tile([P, cols.stop - cols.start], F32, name="a_" + tag, tag=tag)
            nc.tensor.matmul_mx(
                out=bank[:], lhsT=wq[0][:].bitcast(FP8X4), lhsT_scale=wq[1][:], rhs=xw_g[:, cols].bitcast(FP8X4), rhs_scale=xs_g[:, cols], start=True, stop=True
            )
            return bank

        level = []
        for t in range(PACK):
            lv = sb.tile([P, C], F32, name="level%d" % t)
            nc.scalar.activation(out=lv[:], in_=tl_rows[t][:].indirect(l5[:]), func=COPY, scale=sl_t[:, t : t + 1])
            level.append(lv)

        a_rows = [sb.tile([P, J], F32, name="a_rows%d" % t) for t in range(PACK)]
        for t in range(PACK):
            nc.vector.tensor_copy(out=woven[:, t, P // 2 :, 2:4], in_=dealt(wc_high[1])[:, t])
            wq = quantise_wc(woven[:, t], t)
            pieces = [slice(0, J // 2), slice(J // 2, J)] if t == 0 else [slice(0, J)]
            for cols in pieces:
                bank = first_product(wq, cols, "bank%d" % (t if cols.start == 0 else PACK))
                nc.vector.tensor_copy(out=a_rows[t][:, cols], in_=bank[:])

        ws = spread_scale_rows(ws_staged, "ws", "xw_g")
        h1 = sb.tile([P, PACK, O], F32, name="h1", tag="tl3")
        hid_head = sb.tile([P, HEAD, PACK], BF16, name="hid_head", align_bytes=64)
        rest_planes = sb.tile([P, PACK, C - HEAD], BF16, name="rest_planes")

        def gather_slots(t):
            nc.scalar.activation(out=h1[:, t, :], in_=a_rows[t][:].indirect(l3[:]), func=COPY, scale=sa_t[:, t : t + 1])

        gather_slots(0)
        for t in range(PACK):
            if t + 1 < PACK:
                gather_slots(t + 1)
            nc.scalar.activation(out=pw[t][:].indirect(l4[:]), in_=h1[:, t, :], func=COPY)
            nc.vector.tensor_tensor(out=hid_head[:, :, t], in0=pw[t][:, :HEAD], in1=level[t][:, :HEAD], op=ALU.max)
            nc.vector.tensor_tensor(out=rest_planes[:, t, :], in0=pw[t][:, HEAD:], in1=level[t][:, HEAD:], op=ALU.max)

        def second_product(hid, c0, c1, runs, tags):
            width = c1 - c0
            codes = sb.tile([P, width], U32, name="hid_codes%d" % c0, align_bytes=64)
            scales = sb.tile([P, width], U8, name="hid_scales%d" % c0, align_bytes=64)
            for r0, r1 in runs:
                nc.vector.quantize_mx(
                    out=codes[:, r0:r1].bitcast(FP8X4), scales=scales[:, r0:r1], in_=hid[:, r0:r1, :].rearrange("p c t -> p (c t)")
                )
            for b in range(N // P):
                bank = psum.tile([P, width], F32, name="p_bank%d_%d" % (c0, b), tag=tags[b])
                for r0, r1 in runs:
                    nc.tensor.matmul_mx(
                        out=bank[:, r0:r1],
                        lhsT=ww[:, b * P : (b + 1) * P].bitcast(FP8X4),
                        lhsT_scale=ws[:, b * P : (b + 1) * P],
                        rhs=codes[:, r0:r1].bitcast(FP8X4),
                        rhs_scale=scales[:, r0:r1],
                        start=True,
                        stop=True,
                    )
                m0 = sb.tile([P, width], F32, name="m0_%d_%d" % (c0, b))
                m1 = sb.tile([P, width], F32, name="m1_%d_%d" % (c0, b))
                nc.vector.tensor_scalar_max(out=m0[:], in0=bank[:], scalar1=0.0)
                nc.vector.tensor_scalar(out=m1[:], in0=bank[:], scalar1=-1.0, scalar2=0.0, op0=ALU.mult, op1=ALU.max)
                nc.scalar.activation(out=m2[b][:].indirect(l6[:, c0 // 16 : c1 // 16]), in_=m0[:], func=COPY)
                nc.scalar.activation(out=m3[b][:].indirect(l7[:, c0 // 16 : c1 // 16]), in_=m1[:], func=COPY)

        second_product(hid_head, 0, HEAD, [(0, HEAD)], ["bank5", "bank6"])
        hid_rest = sb.tile([P, C - HEAD, PACK], BF16, name="hid_rest", align_bytes=64)
        nc.vector.tensor_copy(out=hid_rest[:], in_=rest_planes[:].rearrange("p t c -> p c t"))
        second_product(hid_rest, HEAD, C, [(0, 64), (64, 192)], ["bank7", "bank0"])

        for b in range(N // P):
            for half, queue in enumerate((nc.sync, nc.scalar)):
                cols = slice(half * U // 2, (half + 1) * U // 2)
                y = sb.tile([P, U // 2], F32, name="y%d_%d" % (b, half))
                nc.vector.tensor_sub(out=y[:], in0=m2[b][:, cols], in1=m3[b][:, cols])
                (queue if b == N // P - 1 else nc.sync).dma_start(out=out[b * P : (b + 1) * P, cols], in_=y[:])
